import numpy as np
import ml_dtypes


def mxq(x, axis, fmt="e4m3"):
    dtype, down = {"e4m3": (ml_dtypes.float8_e4m3fn, 7), "e5m2": (ml_dtypes.float8_e5m2, 14)}[fmt]
    v = np.moveaxis(np.asarray(x, np.float32).astype(ml_dtypes.bfloat16).astype(np.float64), axis, -1)
    blocks = v.reshape(v.shape[:-1] + (-1, 32))
    amax = np.abs(blocks).max(-1, keepdims=True)
    byte = np.maximum(np.where(amax > 0, np.frexp(amax)[1] - 1 + 127, 0) - down, 1)
    scale = np.exp2(byte - 127.0)
    codes = (blocks / scale).astype(np.float32).astype(dtype).astype(np.float64)
    return np.moveaxis((codes * scale).reshape(v.shape), -1, axis)


WIDE = False


def mx_kscale(k):
    if not WIDE:
        return np.ones(k)
    levels = np.array([10, -10, 5, -5, 0])
    if k % 512:
        return np.exp2(np.random.permutation(np.resize(levels, k // 32))).repeat(32)
    a = np.empty((k // 512, 16))
    for p in range(k // 512):
        a[p, :8] = np.random.permutation(np.resize(levels, 8))
        for g in range(8):
            far = levels[np.abs(levels - a[p, g]) >= 10]
            a[p, g + 8] = far[np.random.randint(len(far))]
    return np.exp2(a.ravel()).repeat(32)


def f64(x):
    return np.asarray(x).astype(np.float64)


def striped(idx):
    return np.tile(idx.reshape(-1, 16).T, (8, 1)).astype(np.uint16)


def unstriped(offs):
    return offs[:16].T.reshape(-1).astype(np.int64)


E2M1 = np.array([0.0, 0.5, 1.0, 1.5, 2.0, 3.0, 4.0, 6.0, -0.0, -0.5, -1.0, -1.5, -2.0, -3.0, -4.0, -6.0])


def pack_weight(w, fmt):
    k, n = w.shape
    w = f64(np.asarray(w, np.float32).astype(ml_dtypes.bfloat16)).reshape(k // 32, 32, n)
    amax = np.abs(w).max(1)
    if fmt == "e4m3":
        byte = np.frexp(amax)[1] - 1 + 127 - 7
    else:
        mant, ex = np.frexp(amax / 6.0)
        byte = np.where(mant > 0.5, ex, ex - 1) + 127
    byte = np.clip(np.where(amax > 0, byte, 1), 1, 254)
    scaled = (w * np.exp2(127.0 - byte)[:, None, :]).reshape(k, n).astype(np.float32)
    by_word = np.ascontiguousarray(scaled.reshape(k // 512, 128, 4, n).transpose(0, 1, 3, 2))
    if fmt == "e4m3":
        words = by_word.astype(ml_dtypes.float8_e4m3fn).view(np.uint8)
    else:
        c = by_word.astype(ml_dtypes.float4_e2m1fn).view(np.uint8) & 0xF
        words = (c[..., 0::2] | (c[..., 1::2] << 4)).reshape(k // 512, 128, 2 * n)
    return np.ascontiguousarray(words), np.ascontiguousarray(byte.astype(np.uint8).reshape(k // 512, 16, n))


def unpack_weight(words, scales, fmt):
    g, _, n = scales.shape
    words = np.ascontiguousarray(words).reshape(g, 128, n, -1)
    if fmt == "e4m3":
        vals = words.view(ml_dtypes.float8_e4m3fn).astype(np.float64)
    else:
        nib = np.empty((g, 128, n, 4), np.uint8)
        nib[..., 0::2] = words & 0xF
        nib[..., 1::2] = words >> 4
        vals = E2M1[nib]
    vals = vals * np.repeat(np.exp2(scales.astype(np.float64) - 127.0), 8, axis=1)[..., None]
    return vals.transpose(0, 1, 3, 2).reshape(g * 512, n)


def relu(v):
    return np.maximum(v, 0.0)


K, T, E, C, N = 1536, 512, 2, 256, 384
K8 = 512


def by_expert(wq, xq):
    return np.concatenate([wq[e].T @ xq[:, e * C:(e + 1) * C] for e in range(E)], axis=1)


def setup_inputs():
    n = np.random.standard_normal
    s = mx_kscale(K)[:, None]
    w = n((E, K, N)) / np.sqrt(K) / s[None]
    w8 = [pack_weight(m[:K8], "e4m3") for m in w]
    w4 = [pack_weight(m[K8:], "e2m1") for m in w]
    return {
        "xT": (n((K, T)) * s).astype(np.float32),
        "w8_words": np.stack([m[0] for m in w8]),
        "w8_scales": np.stack([m[1] for m in w8]),
        "w4_words": np.stack([m[0] for m in w4]),
        "w4_scales": np.stack([m[1] for m in w4]),
        "b": (0.3 * n((N, E))).astype(np.float32),
        "gate": np.tile(np.random.uniform(0.2, 1.0, E * C), (N, 1)).astype(np.float32),
        "offs": striped(np.random.permutation(T)[:E * C]),
    }


def reference(xT, w8_words, w8_scales, w4_words, w4_scales, b, gate, offs):
    idx = unstriped(offs)
    w = np.stack([np.concatenate([unpack_weight(w8_words[e], w8_scales[e], "e4m3"), unpack_weight(w4_words[e], w4_scales[e], "e2m1")]) for e in range(E)])
    xq = mxq(f64(xT)[:, idx], 0, "e4m3")
    y = by_expert(w, xq)
    y = relu(y + np.repeat(f64(b), C, axis=1))
    out = np.zeros((N, T))
    out[:, idx] = f64(gate) * y
    return out

@@ -1,0 +1,184 @@
+from contextlib import ExitStack
+
+import concourse.mybir as mybir
+
+K, T, E, C, N = 1536, 512, 2, 256, 384
+FLOPS = 2 * K * N * E * C
+
+F32 = mybir.dt.float32
+BF16 = mybir.dt.bfloat16
+U32 = mybir.dt.uint32
+I32 = mybir.dt.int32
+U16 = mybir.dt.uint16
+U8 = mybir.dt.uint8
+FP8X4 = mybir.dt.float8_e4m3fn_x4
+FP4X4 = mybir.dt.float4_e2m1fn_x4
+COPY = mybir.ActivationFunctionType.Copy
+RELU = mybir.ActivationFunctionType.Relu
+MULT = mybir.AluOpType.mult
+
+P = 128
+PACK = 4
+PASSES = 3
+H = 128
+M_TILES = N // P
+LIST = C // 16
+
+
+def tile_moe_pln_lin_relu_kernel(
+    tc, xT, w8_words, w8_scales, w4_words, w4_scales, b, gate, offs, out
+):
+    nc = tc.nc
+    with ExitStack() as ctx:
+        keep = ctx.enter_context(tc.tile_pool(name="keep", bufs=1))
+        psum = ctx.enter_context(tc.psum_pool(name="psum", bufs=1))
+
+        offsets = keep.tile([P, E * C // 16], U16, name="offsets")
+        nc.sync.dma_start(offsets[:], offs)
+
+        raw = [keep.tile([P, PACK, T], F32, name=f"raw{a}", align_bytes=64) for a in range(PASSES)]
+        grouped = [keep.tile([P, T, PACK], BF16, name=f"grouped{a}", align_bytes=64) for a in range(PASSES)]
+        words = [keep.tile([P, T], U32, name=f"words{a}", align_bytes=64) for a in range(PASSES)]
+        bytes01 = keep.tile([P, T], U8, name="bytes01", align_bytes=64)
+        bytes2 = keep.tile([P, T], U8, name="bytes2", align_bytes=64)
+        slot_words = [keep.tile([P, E * C], U32, name=f"slot_words{a}", align_bytes=64) for a in range(PASSES)]
+        slot_bytes01 = keep.tile([P, E * C], U8, name="slot_bytes01", align_bytes=64)
+        slot_bytes2 = keep.tile([P, E * C], U8, name="slot_bytes2", align_bytes=64)
+        w8 = keep.tile([P, E, 4 * N], U8, name="w8", align_bytes=64)
+        w4 = keep.tile([P, E, 2, 2 * N], U8, name="w4", align_bytes=64)
+        wsc = keep.tile([P, 3 * E, N], U8, name="wsc", align_bytes=64)
+        bias = keep.tile([P, M_TILES, E], F32, name="bias", align_bytes=64)
+        gates = [keep.tile([P, E * C], F32, name=f"gates{m}", align_bytes=64) for m in range(M_TILES)]
+        result = [keep.tile([P, T], F32, name=f"result{m}", align_bytes=64) for m in range(M_TILES)]
+        warm = keep.tile([P, 8], F32, name="warm", align_bytes=64)
+
+        nc.gpsimd.memset(bytes01[:], 0)
+        nc.gpsimd.memset(bytes2[:], 0)
+        nc.vector.memset(wsc[:].bitcast(I32), 0)
+        nc.vector.memset(warm[:], 0.0)
+
+        def load_x(a, t0, t1):
+            nc.sync.dma_start(
+                out=raw[a][:, :, t0:t1],
+                in_=xT[512 * a : 512 * (a + 1), t0:t1].rearrange("(p j) t -> p j t", j=PACK),
+            )
+
+        for r in range(4):
+            nc.scalar.dma_start(
+                out=wsc[r:P:32, 0:2, :].bitcast(I32),
+                in_=w8_scales.rearrange("e a (q r) n -> r q (e a) n", r=4)[r].bitcast(I32),
+            )
+            nc.gpsimd.dma_start(
+                out=wsc[r:P:32, 2:6, :].bitcast(I32),
+                in_=w4_scales.rearrange("e a (q r) n -> r q (e a) n", r=4)[r].bitcast(I32),
+            )
+        nc.gpsimd.dma_start(out=bias[:], in_=b.rearrange("(m p) e -> p m e", p=P))
+        for a in range(PASSES):
+            load_x(a, 0, 256)
+            load_x(a, 256, 512)
+        nc.sync.dma_start(
+            out=w8[:].bitcast(I32),
+            in_=w8_words.rearrange("e a p n r -> p (e a) (n r)").bitcast(I32),
+        )
+        nc.sync.dma_start(
+            out=w4[:].bitcast(I32),
+            in_=w4_words.rearrange("e a p c -> p e a c").bitcast(I32),
+        )
+        for m in range(M_TILES):
+            nc.sync.dma_start(out=gates[m][:], in_=gate[P * m : P * (m + 1), :])
+
+        nc.scalar.activation(warm[:, 4:8], warm[:, 0:4], RELU)
+
+        def cast(engine, a, t0, t1):
+            dst = grouped[a][:, t0:t1, :]
+            src = raw[a][:, :, t0:t1].rearrange("p j t -> p t j")
+            if engine == "v":
+                nc.vector.tensor_copy(out=dst, in_=src)
+            else:
+                nc.scalar.activation(dst, src, COPY)
+
+        def quantise(a, t0, t1):
+            plane = bytes01[4:P, t0:t1] if a == 0 else (bytes01 if a == 1 else bytes2)[:, t0:t1]
+            nc.vector.quantize_mx(
+                out=words[a][:, t0:t1].bitcast(FP8X4),
+                scales=plane,
+                in_=grouped[a][:, t0:t1, :].rearrange("p t j -> p (t j)"),
+            )
+
+        def gather(dst, src, e):
+            cols = slice(e * C, (e + 1) * C)
+            nc.vector.tensor_copy(dst[:, cols], src[:].indirect(offsets[:, e * LIST : (e + 1) * LIST]))
+
+        acc = [[psum.tile([P, C], F32, name=f"acc{e}_{m}") for m in range(M_TILES)] for e in range(E)]
+
+        def multiply(e, m, a):
+            n_cols = slice(P * m, P * (m + 1))
+            if a == 0:
+                cols = slice(e * C, (e + 1) * C)
+                nc.tensor.matmul_mx(
+                    out=acc[e][m][:],
+                    lhsT=w8[:, e, 4 * P * m : 4 * P * (m + 1)].bitcast(FP8X4),
+                    lhsT_scale=wsc[:, e, n_cols],
+                    rhs=slot_words[0][:, cols].bitcast(FP8X4),
+                    rhs_scale=slot_bytes01[4:P, cols],
+                    start=True,
+                    stop=False,
+                )
+                return
+            plane = slot_bytes01 if a == 1 else slot_bytes2
+            for h in range(C // H):
+                cols = slice(e * C + h * H, e * C + (h + 1) * H)
+                nc.tensor.matmul_mx(
+                    out=acc[e][m][:, h * H : (h + 1) * H],
+                    lhsT=w4[:, e, a - 1, 2 * P * m : 2 * P * (m + 1)].bitcast(FP4X4),
+                    lhsT_scale=wsc[:, 2 + 2 * e + a - 1, n_cols],
+                    rhs=slot_words[a][:, cols].bitcast(FP8X4),
+                    rhs_scale=plane[:, cols],
+                    start=False,
+                    stop=(a == 2 and h == C // H - 1),
+                )
+
+        def finish(e, m):
+            y = keep.tile([P, C], F32, name=f"y{e}_{m}", align_bytes=64)
+            nc.scalar.activation(y[:], acc[e][m][:], RELU, bias=bias[:, m, e : e + 1])
+            nc.vector.tensor_tensor(
+                result[m][:].indirect(offsets[:, e * LIST : (e + 1) * LIST]),
+                y[:],
+                gates[m][:, e * C : (e + 1) * C],
+                MULT,
+            )
+
+        def prepare(a, t0, t1, split):
+            cast("v", a, t0, split)
+            cast("s", a, split, t1)
+
+        prepare(0, 0, 256, 160)
+        prepare(0, 256, 512, 416)
+        quantise(0, 0, 256)
+        quantise(0, 256, 512)
+        prepare(1, 0, 256, 160)
+        gather(slot_words[0], words[0], 0)
+        prepare(1, 256, 512, 416)
+        quantise(1, 0, 256)
+        gather(slot_words[0], words[0], 1)
+        quantise(1, 256, 512)
+        prepare(2, 0, 256, 64)
+        gather(slot_bytes01, bytes01, 0)
+        gather(slot_words[1], words[1], 0)
+        gather(slot_bytes01, bytes01, 1)
+        prepare(2, 256, 512, 384)
+        quantise(2, 0, 256)
+        gather(slot_words[1], words[1], 1)
+        quantise(2, 256, 512)
+        for e in range(E):
+            gather(slot_words[2], words[2], e)
+            gather(slot_bytes2, bytes2, e)
+            for m in range(M_TILES):
+                multiply(e, m, 0)
+                multiply(e, m, 1)
+            for m in range(M_TILES):
+                multiply(e, m, 2)
+        for e, m in ((0, 0), (0, 1), (1, 0), (0, 2), (1, 1), (1, 2)):
+            finish(e, m)
+            if e == 1:
+                nc.sync.dma_start(out=out[P * m : P * (m + 1), :], in_=result[m][:])

@@ -34,7 +34,6 @@ def tile_moe_pln_lin_relu_kernel(
         psum = ctx.enter_context(tc.psum_pool(name="psum", bufs=1))
 
         offsets = keep.tile([P, E * C // 16], U16, name="offsets")
-        nc.sync.dma_start(offsets[:], offs)
 
         raw = [keep.tile([P, PACK, T], F32, name=f"raw{a}", align_bytes=64) for a in range(PASSES)]
         grouped = [keep.tile([P, T, PACK], BF16, name=f"grouped{a}", align_bytes=64) for a in range(PASSES)]
@@ -64,27 +63,30 @@ def tile_moe_pln_lin_relu_kernel(
             )
 
         for r in range(4):
-            nc.scalar.dma_start(
-                out=wsc[r:P:32, 0:2, :].bitcast(I32),
-                in_=w8_scales.rearrange("e a (q r) n -> r q (e a) n", r=4)[r].bitcast(I32),
-            )
             nc.gpsimd.dma_start(
                 out=wsc[r:P:32, 2:6, :].bitcast(I32),
                 in_=w4_scales.rearrange("e a (q r) n -> r q (e a) n", r=4)[r].bitcast(I32),
             )
-        nc.gpsimd.dma_start(out=bias[:], in_=b.rearrange("(m p) e -> p m e", p=P))
-        for a in range(PASSES):
-            load_x(a, 0, 256)
-            load_x(a, 256, 512)
-        nc.sync.dma_start(
-            out=w8[:].bitcast(I32),
-            in_=w8_words.rearrange("e a p n r -> p (e a) (n r)").bitcast(I32),
-        )
-        nc.sync.dma_start(
-            out=w4[:].bitcast(I32),
-            in_=w4_words.rearrange("e a p c -> p e a c").bitcast(I32),
-        )
-        for m in range(M_TILES):
+        load_x(0, 0, T)
+        nc.sync.dma_start(offsets[:], offs)
+        load_x(1, 0, T)
+        load_x(2, 0, T)
+
+        def load_w(e):
+            nc.sync.dma_start(
+                out=w8[:, e, :].bitcast(I32),
+                in_=w8_words[e, 0].rearrange("p n r -> p (n r)").bitcast(I32),
+            )
+            nc.sync.dma_start(
+                out=w4[:, e].bitcast(I32),
+                in_=w4_words[e].rearrange("a p c -> p a c").bitcast(I32),
+            )
+
+        load_w(0)
+        nc.sync.dma_start(out=bias[:], in_=b.rearrange("(m p) e -> p m e", p=P))
+        nc.sync.dma_start(out=gates[0][:], in_=gate[0:P, :])
+        load_w(1)
+        for m in range(1, M_TILES):
             nc.sync.dma_start(out=gates[m][:], in_=gate[P * m : P * (m + 1), :])
 
         nc.scalar.activation(warm[:, 4:8], warm[:, 0:4], RELU)
@@ -148,27 +150,30 @@ def tile_moe_pln_lin_relu_kernel(
                 MULT,
             )
 
-        def prepare(a, t0, t1, split):
-            cast("v", a, t0, split)
-            cast("s", a, split, t1)
-
-        prepare(0, 0, 256, 160)
-        prepare(0, 256, 512, 416)
+        cast("v", 0, 0, 256)
+        cast("s", 0, 352, 512)
+        cast("v", 0, 256, 352)
         quantise(0, 0, 256)
         quantise(0, 256, 512)
-        prepare(1, 0, 256, 160)
+        for r in range(4):
+            nc.scalar.dma_start(
+                out=wsc[r:P:32, 0:2, :].bitcast(I32),
+                in_=w8_scales.rearrange("e a (q r) n -> r q (e a) n", r=4)[r].bitcast(I32),
+            )
+        cast("s", 1, 0, 256)
         gather(slot_words[0], words[0], 0)
-        prepare(1, 256, 512, 416)
-        quantise(1, 0, 256)
         gather(slot_words[0], words[0], 1)
+        cast("v", 1, 256, 512)
         quantise(1, 256, 512)
-        prepare(2, 0, 256, 64)
-        gather(slot_bytes01, bytes01, 0)
+        quantise(1, 0, 256)
+        cast("s", 2, 0, 256)
+        cast("s", 2, 256, 400)
         gather(slot_words[1], words[1], 0)
-        gather(slot_bytes01, bytes01, 1)
-        prepare(2, 256, 512, 384)
-        quantise(2, 0, 256)
+        gather(slot_bytes01, bytes01, 0)
         gather(slot_words[1], words[1], 1)
+        cast("v", 2, 400, 512)
+        quantise(2, 0, 256)
+        gather(slot_bytes01, bytes01, 1)
         quantise(2, 256, 512)
         for e in range(E):
             gather(slot_words[2], words[2], e)

@@ -67,10 +67,17 @@ def tile_moe_pln_lin_relu_kernel(
                 out=wsc[r:P:32, 2:6, :].bitcast(I32),
                 in_=w4_scales.rearrange("e a (q r) n -> r q (e a) n", r=4)[r].bitcast(I32),
             )
-        load_x(0, 0, T)
+        load_x(0, 0, 256)
+        load_x(0, 256, 512)
         nc.sync.dma_start(offsets[:], offs)
-        load_x(1, 0, T)
-        load_x(2, 0, T)
+        for r in range(4):
+            nc.sync.dma_start(
+                out=wsc[r:P:32, 0:2, :].bitcast(I32),
+                in_=w8_scales.rearrange("e a (q r) n -> r q (e a) n", r=4)[r].bitcast(I32),
+            )
+        for a in range(1, PASSES):
+            load_x(a, 0, 256)
+            load_x(a, 256, 512)
 
         def load_w(e):
             nc.sync.dma_start(
@@ -92,8 +99,8 @@ def tile_moe_pln_lin_relu_kernel(
         nc.scalar.activation(warm[:, 4:8], warm[:, 0:4], RELU)
 
         def cast(engine, a, t0, t1):
-            dst = grouped[a][:, t0:t1, :]
-            src = raw[a][:, :, t0:t1].rearrange("p j t -> p t j")
+            dst = grouped[a][:, t0:t1, :].rearrange("p (c i) j -> p c j i", i=4)
+            src = raw[a][:, :, t0:t1].rearrange("p j (c i) -> p c j i", i=4)
             if engine == "v":
                 nc.vector.tensor_copy(out=dst, in_=src)
             else:
@@ -150,31 +157,28 @@ def tile_moe_pln_lin_relu_kernel(
                 MULT,
             )
 
-        cast("v", 0, 0, 256)
-        cast("s", 0, 352, 512)
-        cast("v", 0, 256, 352)
+        cast("v", 0, 0, 160)
+        cast("s", 0, 160, 256)
         quantise(0, 0, 256)
+        cast("v", 0, 256, 432)
+        cast("s", 0, 432, 512)
         quantise(0, 256, 512)
-        for r in range(4):
-            nc.scalar.dma_start(
-                out=wsc[r:P:32, 0:2, :].bitcast(I32),
-                in_=w8_scales.rearrange("e a (q r) n -> r q (e a) n", r=4)[r].bitcast(I32),
-            )
         cast("s", 1, 0, 256)
         gather(slot_words[0], words[0], 0)
+        cast("v", 1, 256, 432)
+        cast("s", 1, 432, 512)
         gather(slot_words[0], words[0], 1)
-        cast("v", 1, 256, 512)
-        quantise(1, 256, 512)
         quantise(1, 0, 256)
+        quantise(1, 256, 512)
         cast("s", 2, 0, 256)
-        cast("s", 2, 256, 400)
+        cast("s", 2, 256, 448)
         gather(slot_words[1], words[1], 0)
         gather(slot_bytes01, bytes01, 0)
         gather(slot_words[1], words[1], 1)
-        cast("v", 2, 400, 512)
+        cast("v", 2, 448, 512)
         quantise(2, 0, 256)
-        gather(slot_bytes01, bytes01, 1)
         quantise(2, 256, 512)
+        gather(slot_bytes01, bytes01, 1)
         for e in range(E):
             gather(slot_words[2], words[2], e)
             gather(slot_bytes2, bytes2, e)

@@ -62,22 +62,18 @@ def tile_moe_pln_lin_relu_kernel(
                 in_=xT[512 * a : 512 * (a + 1), t0:t1].rearrange("(p j) t -> p j t", j=PACK),
             )
 
-        for r in range(4):
-            nc.gpsimd.dma_start(
-                out=wsc[r:P:32, 2:6, :].bitcast(I32),
-                in_=w4_scales.rearrange("e a (q r) n -> r q (e a) n", r=4)[r].bitcast(I32),
-            )
         load_x(0, 0, 256)
         load_x(0, 256, 512)
         nc.sync.dma_start(offsets[:], offs)
+        load_x(1, 0, 256)
+        load_x(1, 256, 512)
         for r in range(4):
             nc.sync.dma_start(
                 out=wsc[r:P:32, 0:2, :].bitcast(I32),
                 in_=w8_scales.rearrange("e a (q r) n -> r q (e a) n", r=4)[r].bitcast(I32),
             )
-        for a in range(1, PASSES):
-            load_x(a, 0, 256)
-            load_x(a, 256, 512)
+        load_x(2, 0, 256)
+        load_x(2, 256, 512)
 
         def load_w(e):
             nc.sync.dma_start(
@@ -90,6 +86,11 @@ def tile_moe_pln_lin_relu_kernel(
             )
 
         load_w(0)
+        for r in range(4):
+            nc.sync.dma_start(
+                out=wsc[r:P:32, 2:6, :].bitcast(I32),
+                in_=w4_scales.rearrange("e a (q r) n -> r q (e a) n", r=4)[r].bitcast(I32),
+            )
         nc.sync.dma_start(out=bias[:], in_=b.rearrange("(m p) e -> p m e", p=P))
         nc.sync.dma_start(out=gates[0][:], in_=gate[0:P, :])
         load_w(1)
@@ -157,8 +158,7 @@ def tile_moe_pln_lin_relu_kernel(
                 MULT,
             )
 
-        cast("v", 0, 0, 160)
-        cast("s", 0, 160, 256)
+        cast("v", 0, 0, 256)
         quantise(0, 0, 256)
         cast("v", 0, 256, 432)
         cast("s", 0, 432, 512)

@@ -85,12 +85,12 @@ def tile_moe_pln_lin_relu_kernel(
                 in_=w4_words[e].rearrange("a p c -> p a c").bitcast(I32),
             )
 
-        load_w(0)
         for r in range(4):
             nc.sync.dma_start(
                 out=wsc[r:P:32, 2:6, :].bitcast(I32),
                 in_=w4_scales.rearrange("e a (q r) n -> r q (e a) n", r=4)[r].bitcast(I32),
             )
+        load_w(0)
         nc.sync.dma_start(out=bias[:], in_=b.rearrange("(m p) e -> p m e", p=P))
         nc.sync.dma_start(out=gates[0][:], in_=gate[0:P, :])
         load_w(1)
@@ -184,6 +184,7 @@ def tile_moe_pln_lin_relu_kernel(
             gather(slot_bytes2, bytes2, e)
             for m in range(M_TILES):
                 multiply(e, m, 0)
+            for m in range(M_TILES):
                 multiply(e, m, 1)
             for m in range(M_TILES):
                 multiply(e, m, 2)

from contextlib import ExitStack

import concourse.mybir as mybir

K, T, E, C, N = 1536, 512, 2, 256, 384
FLOPS = 2 * K * N * E * C

F32 = mybir.dt.float32
BF16 = mybir.dt.bfloat16
U32 = mybir.dt.uint32
I32 = mybir.dt.int32
U16 = mybir.dt.uint16
U8 = mybir.dt.uint8
FP8X4 = mybir.dt.float8_e4m3fn_x4
FP4X4 = mybir.dt.float4_e2m1fn_x4
COPY = mybir.ActivationFunctionType.Copy
RELU = mybir.ActivationFunctionType.Relu
MULT = mybir.AluOpType.mult

P = 128
PACK = 4
PASSES = 3
H = 128
M_TILES = N // P
LIST = C // 16


def tile_moe_pln_lin_relu_kernel(
    tc, xT, w8_words, w8_scales, w4_words, w4_scales, b, gate, offs, out
):
    nc = tc.nc
    with ExitStack() as ctx:
        keep = ctx.enter_context(tc.tile_pool(name="keep", bufs=1))
        psum = ctx.enter_context(tc.psum_pool(name="psum", bufs=1))

        offsets = keep.tile([P, E * C // 16], U16, name="offsets")

        raw = [keep.tile([P, PACK, T], F32, name=f"raw{a}", align_bytes=64) for a in range(PASSES)]
        grouped = [keep.tile([P, T, PACK], BF16, name=f"grouped{a}", align_bytes=64) for a in range(PASSES)]
        words = [keep.tile([P, T], U32, name=f"words{a}", align_bytes=64) for a in range(PASSES)]
        bytes01 = keep.tile([P, T], U8, name="bytes01", align_bytes=64)
        bytes2 = keep.tile([P, T], U8, name="bytes2", align_bytes=64)
        slot_words = [keep.tile([P, E * C], U32, name=f"slot_words{a}", align_bytes=64) for a in range(PASSES)]
        slot_bytes01 = keep.tile([P, E * C], U8, name="slot_bytes01", align_bytes=64)
        slot_bytes2 = keep.tile([P, E * C], U8, name="slot_bytes2", align_bytes=64)
        w8 = keep.tile([P, E, 4 * N], U8, name="w8", align_bytes=64)
        w4 = keep.tile([P, E, 2, 2 * N], U8, name="w4", align_bytes=64)
        wsc = keep.tile([P, 3 * E, N], U8, name="wsc", align_bytes=64)
        bias = keep.tile([P, M_TILES, E], F32, name="bias", align_bytes=64)
        gates = [keep.tile([P, E * C], F32, name=f"gates{m}", align_bytes=64) for m in range(M_TILES)]
        result = [keep.tile([P, T], F32, name=f"result{m}", align_bytes=64) for m in range(M_TILES)]
        warm = keep.tile([P, 8], F32, name="warm", align_bytes=64)

        nc.gpsimd.memset(bytes01[:], 0)
        nc.gpsimd.memset(bytes2[:], 0)
        nc.vector.memset(wsc[:].bitcast(I32), 0)
        nc.vector.memset(warm[:], 0.0)

        def load_x(a, t0, t1):
            nc.sync.dma_start(
                out=raw[a][:, :, t0:t1],
                in_=xT[512 * a : 512 * (a + 1), t0:t1].rearrange("(p j) t -> p j t", j=PACK),
            )

        load_x(0, 0, 256)
        load_x(0, 256, 512)
        nc.sync.dma_start(offsets[:], offs)
        load_x(1, 0, 256)
        load_x(1, 256, 512)
        for r in range(4):
            nc.sync.dma_start(
                out=wsc[r:P:32, 0:2, :].bitcast(I32),
                in_=w8_scales.rearrange("e a (q r) n -> r q (e a) n", r=4)[r].bitcast(I32),
            )
        load_x(2, 0, 256)
        load_x(2, 256, 512)

        def load_w(e):
            nc.sync.dma_start(
                out=w8[:, e, :].bitcast(I32),
                in_=w8_words[e, 0].rearrange("p n r -> p (n r)").bitcast(I32),
            )
            nc.sync.dma_start(
                out=w4[:, e].bitcast(I32),
                in_=w4_words[e].rearrange("a p c -> p a c").bitcast(I32),
            )

        for r in range(4):
            nc.sync.dma_start(
                out=wsc[r:P:32, 2:6, :].bitcast(I32),
                in_=w4_scales.rearrange("e a (q r) n -> r q (e a) n", r=4)[r].bitcast(I32),
            )
        load_w(0)
        nc.sync.dma_start(out=bias[:], in_=b.rearrange("(m p) e -> p m e", p=P))
        nc.sync.dma_start(out=gates[0][:], in_=gate[0:P, :])
        load_w(1)
        for m in range(1, M_TILES):
            nc.sync.dma_start(out=gates[m][:], in_=gate[P * m : P * (m + 1), :])

        nc.scalar.activation(warm[:, 4:8], warm[:, 0:4], RELU)

        def cast(engine, a, t0, t1):
            dst = grouped[a][:, t0:t1, :].rearrange("p (c i) j -> p c j i", i=4)
            src = raw[a][:, :, t0:t1].rearrange("p j (c i) -> p c j i", i=4)
            if engine == "v":
                nc.vector.tensor_copy(out=dst, in_=src)
            else:
                nc.scalar.activation(dst, src, COPY)

        def quantise(a, t0, t1):
            plane = bytes01[4:P, t0:t1] if a == 0 else (bytes01 if a == 1 else bytes2)[:, t0:t1]
            nc.vector.quantize_mx(
                out=words[a][:, t0:t1].bitcast(FP8X4),
                scales=plane,
                in_=grouped[a][:, t0:t1, :].rearrange("p t j -> p (t j)"),
            )

        def gather(dst, src, e):
            cols = slice(e * C, (e + 1) * C)
            nc.vector.tensor_copy(dst[:, cols], src[:].indirect(offsets[:, e * LIST : (e + 1) * LIST]))

        acc = [[psum.tile([P, C], F32, name=f"acc{e}_{m}") for m in range(M_TILES)] for e in range(E)]

        def multiply(e, m, a):
            n_cols = slice(P * m, P * (m + 1))
            if a == 0:
                cols = slice(e * C, (e + 1) * C)
                nc.tensor.matmul_mx(
                    out=acc[e][m][:],
                    lhsT=w8[:, e, 4 * P * m : 4 * P * (m + 1)].bitcast(FP8X4),
                    lhsT_scale=wsc[:, e, n_cols],
                    rhs=slot_words[0][:, cols].bitcast(FP8X4),
                    rhs_scale=slot_bytes01[4:P, cols],
                    start=True,
                    stop=False,
                )
                return
            plane = slot_bytes01 if a == 1 else slot_bytes2
            for h in range(C // H):
                cols = slice(e * C + h * H, e * C + (h + 1) * H)
                nc.tensor.matmul_mx(
                    out=acc[e][m][:, h * H : (h + 1) * H],
                    lhsT=w4[:, e, a - 1, 2 * P * m : 2 * P * (m + 1)].bitcast(FP4X4),
                    lhsT_scale=wsc[:, 2 + 2 * e + a - 1, n_cols],
                    rhs=slot_words[a][:, cols].bitcast(FP8X4),
                    rhs_scale=plane[:, cols],
                    start=False,
                    stop=(a == 2 and h == C // H - 1),
                )

        def finish(e, m):
            y = keep.tile([P, C], F32, name=f"y{e}_{m}", align_bytes=64)
            nc.scalar.activation(y[:], acc[e][m][:], RELU, bias=bias[:, m, e : e + 1])
            nc.vector.tensor_tensor(
                result[m][:].indirect(offsets[:, e * LIST : (e + 1) * LIST]),
                y[:],
                gates[m][:, e * C : (e + 1) * C],
                MULT,
            )

        cast("v", 0, 0, 256)
        quantise(0, 0, 256)
        cast("v", 0, 256, 432)
        cast("s", 0, 432, 512)
        quantise(0, 256, 512)
        cast("s", 1, 0, 256)
        gather(slot_words[0], words[0], 0)
        cast("v", 1, 256, 432)
        cast("s", 1, 432, 512)
        gather(slot_words[0], words[0], 1)
        quantise(1, 0, 256)
        quantise(1, 256, 512)
        cast("s", 2, 0, 256)
        cast("s", 2, 256, 448)
        gather(slot_words[1], words[1], 0)
        gather(slot_bytes01, bytes01, 0)
        gather(slot_words[1], words[1], 1)
        cast("v", 2, 448, 512)
        quantise(2, 0, 256)
        quantise(2, 256, 512)
        gather(slot_bytes01, bytes01, 1)
        for e in range(E):
            gather(slot_words[2], words[2], e)
            gather(slot_bytes2, bytes2, e)
            for m in range(M_TILES):
                multiply(e, m, 0)
            for m in range(M_TILES):
                multiply(e, m, 1)
            for m in range(M_TILES):
                multiply(e, m, 2)
        for e, m in ((0, 0), (0, 1), (1, 0), (0, 2), (1, 1), (1, 2)):
            finish(e, m)
            if e == 1:
                nc.sync.dma_start(out=out[P * m : P * (m + 1), :], in_=result[m][:])
